import numpy as np
import ml_dtypes


def mxq(x, axis, fmt="e4m3"):
    dtype, down = {"e4m3": (ml_dtypes.float8_e4m3fn, 7), "e5m2": (ml_dtypes.float8_e5m2, 14)}[fmt]
    v = np.moveaxis(np.asarray(x, np.float32).astype(ml_dtypes.bfloat16).astype(np.float64), axis, -1)
    blocks = v.reshape(v.shape[:-1] + (-1, 32))
    amax = np.abs(blocks).max(-1, keepdims=True)
    byte = np.maximum(np.where(amax > 0, np.frexp(amax)[1] - 1 + 127, 0) - down, 1)
    scale = np.exp2(byte - 127.0)
    codes = (blocks / scale).astype(np.float32).astype(dtype).astype(np.float64)
    return np.moveaxis((codes * scale).reshape(v.shape), -1, axis)


WIDE = False


def mx_kscale(k):
    if not WIDE:
        return np.ones(k)
    levels = np.array([10, -10, 5, -5, 0])
    if k % 512:
        return np.exp2(np.random.permutation(np.resize(levels, k // 32))).repeat(32)
    a = np.empty((k // 512, 16))
    for p in range(k // 512):
        a[p, :8] = np.random.permutation(np.resize(levels, 8))
        for g in range(8):
            far = levels[np.abs(levels - a[p, g]) >= 10]
            a[p, g + 8] = far[np.random.randint(len(far))]
    return np.exp2(a.ravel()).repeat(32)


def f64(x):
    return np.asarray(x).astype(np.float64)


def striped(idx):
    return np.tile(idx.reshape(-1, 16).T, (8, 1)).astype(np.uint16)


def unstriped(offs):
    return offs[:16].T.reshape(-1).astype(np.int64)


def striped8(idx):
    return np.concatenate([x.reshape(-1, 16).T for x in idx]).astype(np.uint16)


def runs(offs, k):
    lists = np.stack([offs[16 * r : 16 * r + 16].T.reshape(-1) for r in range(8)]).astype(np.int64)
    return lists[np.arange(k) % 512 // 64]


def pack_weight(w):
    k, n = w.shape
    w = f64(np.asarray(w, np.float32).astype(ml_dtypes.bfloat16)).reshape(k // 32, 32, n)
    amax = np.abs(w).max(1)
    byte = np.clip(np.where(amax > 0, np.frexp(amax)[1] - 1 + 127 - 7, 1), 1, 254)
    scaled = (w * np.exp2(127.0 - byte)[:, None, :]).reshape(k, n).astype(np.float32)
    words = np.ascontiguousarray(scaled.reshape(k // 512, 128, 4, n).transpose(0, 1, 3, 2)).astype(ml_dtypes.float8_e4m3fn).view(np.uint8)
    return words, np.ascontiguousarray(byte.astype(np.uint8).reshape(k // 512, 16, n))


def unpack_weight(words, scales):
    g, p, n, _ = words.shape
    vals = np.ascontiguousarray(words).view(ml_dtypes.float8_e4m3fn).astype(np.float64) * np.repeat(np.exp2(scales.astype(np.float64) - 127.0), 8, axis=1)[..., None]
    return vals.transpose(0, 1, 3, 2).reshape(g * 512, n)


def sigmoid(v):
    return 1.0 / (1.0 + np.exp(-np.maximum(v, -700.0)))

def planes(y):
    n, m = y.shape
    v = y.astype(np.float32).astype(ml_dtypes.bfloat16).astype(np.float64).reshape(n // 32, 32, m)
    top = np.abs(v).max(1)
    byte = np.clip(np.where(top > 0, np.frexp(top)[1] - 1 + 127 - 7, 1), 1, 254)
    codes = (v * np.exp2(127.0 - byte)[:, None, :]).reshape(n, m).astype(np.float32).astype(ml_dtypes.float8_e4m3fn).view(np.uint8)
    words = codes.reshape(n // 512, 128, 4, m).transpose(0, 1, 3, 2)
    return np.ascontiguousarray(words), np.ascontiguousarray(byte.astype(np.uint8).reshape(n // 512, 16, m))


K, T, S, N, G, H = 512, 1024, 512, 512, 2048, 512


def setup_inputs():
    n = np.random.standard_normal
    s = mx_kscale(K)[:, None]
    u = mx_kscale(S)
    packed_xT = pack_weight(n((K, T)) * s)
    packed_dT = pack_weight(n((K, G)) / s)
    packed_w1 = pack_weight(n((H, N)) / np.sqrt(2 * H) / u[:, None])
    packed_w2 = pack_weight(n((K, N)) / np.sqrt(2 * K) / s)
    return {
        "x_words": packed_xT[0],
        "x_scales": packed_xT[1],
        "d_words": packed_dT[0],
        "d_scales": packed_dT[1],
        "gn": (np.random.uniform(0.5, 1.5, (H, 1)) * u[:, None]).astype(np.float32),
        "w1_words": packed_w1[0],
        "w1_scales": packed_w1[1],
        "w2_words": packed_w2[0],
        "w2_scales": packed_w2[1],
        "sl": np.random.uniform(1.5, 2.5, (N, 1)).astype(np.float32),
        "lo": np.random.uniform(-1.2, -0.4, (N, 1)).astype(np.float32),
        "hi": np.random.uniform(0.4, 1.2, (N, 1)).astype(np.float32),
        "offs": striped(np.random.permutation(T)[:S]),
        "k1": striped8(np.random.randint(0, G, (8, H))),
        "n1": striped(np.random.permutation(S)),
        "n2": striped(np.random.permutation(S)),
        "two": striped(np.random.permutation(T)[:S]),
        "n3": striped(np.random.permutation(S)),
    }


def reference(x_words, x_scales, d_words, d_scales, gn, w1_words, w1_scales, w2_words, w2_scales, sl, lo, hi, offs, k1, n1, n2, two, n3):
    d_k1 = unpack_weight(d_words, d_scales)[np.arange(K)[:, None], runs(k1, K)]
    xq = unpack_weight(x_words, x_scales)[:, unstriped(offs)]
    h = 0.0625 * (d_k1.T @ xq)
    z = f64(gn) * (h[:, unstriped(n1)] / (np.abs(h) + np.abs(h[:, unstriped(n2)]) + 0.5))
    x_two = unpack_weight(x_words, x_scales)[:, unstriped(two)]
    h2 = unpack_weight(w1_words, w1_scales).T @ mxq(z, 0, "e4m3") + unpack_weight(w2_words, w2_scales).T @ x_two
    sg = sigmoid(f64(sl) * (h2[:, unstriped(n3)] - f64(lo)))
    sg2 = sigmoid(f64(sl) * (h2[:, unstriped(n3)] - f64(hi)))
    out_0 = h2 * (sg - sg2)
    return (out_0,) + planes(out_0)

@@ -1,0 +1,245 @@
+from contextlib import ExitStack
+
+import concourse.mybir as mybir
+
+K, T, S, N, G, H = 512, 1024, 512, 512, 2048, 512
+FLOPS = 3 * 2 * 512 * 512 * 512
+
+F32 = mybir.dt.float32
+BF16 = mybir.dt.bfloat16
+I32 = mybir.dt.int32
+U32 = mybir.dt.uint32
+U16 = mybir.dt.uint16
+U8 = mybir.dt.uint8
+FP8X4 = mybir.dt.float8_e4m3fn_x4
+ALU = mybir.AluOpType
+ACT = mybir.ActivationFunctionType
+
+P = 128
+PACK = 4
+Z_CHUNKS = ((0, 256), (256, 128), (384, 128))
+VECTOR_CHUNK = 1
+GAINS_ON_VECTOR = 2
+Y_CHUNKS = ((0, 256), (256, 128), (384, 128))
+
+
+def words_view(dram):
+    return dram[0].rearrange("p n t -> p (n t)").bitcast(I32)
+
+
+def entries(offsets, start, count):
+    return offsets[:, start // 16 : (start + count) // 16]
+
+
+def deal(engine_copy, dealt, plain):
+    engine_copy(dealt.rearrange("p (t m) -> p m t", t=PACK), plain.rearrange("p (m t) -> p m t", t=PACK))
+
+
+def tile_picked_pqmixnorm2ebd_none_po_kernel(
+    tc, x_words, x_scales, d_words, d_scales, gn, w1_words, w1_scales, w2_words, w2_scales, sl, lo, hi,
+    offs, k1, n1, n2, two, n3, out_0, out_1, out_2,
+):
+    nc = tc.nc
+    with ExitStack() as ctx:
+        keep = ctx.enter_context(tc.tile_pool(name="keep", bufs=1))
+        psum = ctx.enter_context(tc.psum_pool(name="psum", bufs=1))
+
+        def new(shape, dtype, name):
+            return keep.tile(shape, dtype, name=name, align_bytes=64)
+
+        lists = {name: new([P, 32], U16, "list_" + name) for name in ("k1", "offs", "two", "n2", "n1", "n3")}
+        d_table_w = keep.tile([P, G], U32, name="d_table_w", tag="d_then_w", align_bytes=64)
+        d_table_s = keep.tile([P, G], U8, name="d_table_s", tag="d_scales_then_w", align_bytes=64)
+        x_table_w = new([P, T], U32, "x_table_w")
+        x_table_s = new([P, T], U8, "x_table_s")
+        gn_sb = new([P, PACK], F32, "gn_sb")
+        sl_sb = new([P, PACK], F32, "sl_sb")
+        lo_sb = new([P, PACK], F32, "lo_sb")
+        hi_sb = new([P, PACK], F32, "hi_sb")
+
+        nc.vector.memset(x_table_s[:].bitcast(I32), 0)
+
+        nc.sync.dma_start(lists["k1"][:], k1)
+        nc.sync.dma_start(d_table_s[:].bitcast(I32), d_scales[0].bitcast(I32).unsqueeze(1).to_broadcast([16, 8, G // 4]))
+        nc.sync.dma_start(lists["offs"][:], offs)
+        nc.sync.dma_start(d_table_w[:].bitcast(I32), words_view(d_words))
+        nc.sync.dma_start(x_table_w[:].bitcast(I32), words_view(x_words))
+        for r in range(4):
+            nc.scalar.dma_start(x_table_s[r:P:32, :].bitcast(I32), x_scales[0][r:16:4, :].bitcast(I32))
+        nc.sync.dma_start(lists["two"][:], two)
+        for name, src in (("n2", n2), ("n1", n1), ("n3", n3)):
+            nc.sync.dma_start(lists[name][:], src)
+        for tile, src in ((gn_sb, gn), (sl_sb, sl), (lo_sb, lo), (hi_sb, hi)):
+            nc.gpsimd.dma_start(tile[:], src.rearrange("(p t) o -> p (t o)", t=PACK))
+
+        d_pick_s = keep.tile([P, H], U8, name="d_pick_s", tag="d_pick", align_bytes=64)
+        d_dealt_s = new([P, H], U8, "d_dealt_s")
+        d_dealt_w = new([P, H], U32, "d_dealt_w")
+        xq_w = new([P, S], U32, "xq_w")
+        xq_s = new([P, S], U8, "xq_s")
+        nc.vector.tensor_copy(d_pick_s[:], d_table_s[:].indirect(lists["k1"][:]))
+        deal(nc.vector.tensor_copy, d_dealt_s[:], d_pick_s[:])
+        for r in range(1, 4):
+            queue = (nc.sync, nc.scalar)[r % 2]
+            queue.dma_start(d_dealt_s[r:P:32, :].bitcast(I32), d_dealt_s[8 * r : P : 32, :].bitcast(I32))
+        w_plain = keep.tile([P, 2 * N], U32, name="w_plain", tag="d_scales_then_w", align_bytes=64)
+        w2_plain, w1_plain = w_plain[:, :N], w_plain[:, N:]
+        nc.sync.dma_start(w2_plain.bitcast(I32), words_view(w2_words))
+        nc.sync.dma_start(w1_plain.bitcast(I32), words_view(w1_words))
+        d_pick_w = keep.tile([P, H], U32, name="d_pick_w", tag="d_pick", align_bytes=64)
+        nc.vector.tensor_copy(d_pick_w[:], d_table_w[:].indirect(lists["k1"][:]))
+        nc.vector.tensor_copy(xq_w[:], x_table_w[:].indirect(lists["offs"][:]))
+        deal(nc.vector.tensor_copy, d_dealt_w[:], d_pick_w[:])
+        nc.vector.tensor_copy(xq_s[:], x_table_s[:].indirect(lists["offs"][:]))
+
+        w_plain_s = keep.tile([P, N], U8, name="w_plain_s", tag="d_then_w", align_bytes=64)
+        nc.gpsimd.memset(w_plain_s[:].bitcast(I32), 0)
+        for first_row, scales in ((4, w2_scales), (0, w1_scales)):
+            for r in range(4):
+                nc.sync.dma_start(w_plain_s[first_row + r : P : 32, :].bitcast(I32), scales[0][r:16:4, :].bitcast(I32))
+
+        w1_dealt = new([P, N], U32, "w1_dealt")
+        w2_dealt = new([P, N], U32, "w2_dealt")
+        w_dealt_s = new([P, N], U8, "w_dealt_s")
+        deal(nc.scalar.copy, w2_dealt[:], w2_plain)
+        deal(nc.scalar.copy, w1_dealt[:], w1_plain)
+
+        h_bank = [psum.tile([P, S], F32, name="h_bank%d" % t, tag="bank%d" % t) for t in range(PACK)]
+        for t in range(PACK):
+            cols = slice(t * P, (t + 1) * P)
+            nc.tensor.matmul_mx(
+                out=h_bank[t][:], lhsT=d_dealt_w[:, cols].bitcast(FP8X4), lhsT_scale=d_dealt_s[:, cols],
+                rhs=xq_w[:].bitcast(FP8X4), rhs_scale=xq_s[:], start=True, stop=True,
+            )
+
+        x2_w = new([P, S], U32, "x2_w")
+        x2_s = new([P, S], U8, "x2_s")
+        nc.vector.tensor_copy(x2_w[:], x_table_w[:].indirect(lists["two"][:]))
+        nc.vector.tensor_copy(x2_s[:], x_table_s[:].indirect(lists["two"][:]))
+        minus_sl = new([P, PACK], F32, "minus_sl")
+        bias_lo = new([P, PACK], F32, "bias_lo")
+        bias_hi = new([P, PACK], F32, "bias_hi")
+        nc.gpsimd.tensor_scalar(minus_sl[:], sl_sb[:], -1.0, 0.0, ALU.mult, ALU.add)
+        nc.gpsimd.tensor_tensor(bias_lo[:], minus_sl[:], lo_sb[:], ALU.mult)
+        nc.gpsimd.tensor_tensor(bias_hi[:], minus_sl[:], hi_sb[:], ALU.mult)
+
+        size = [new([P, S], F32, "size%d" % t) for t in range(PACK)]
+        size_again = [new([P, S], F32, "size_again%d" % t) for t in range(PACK)]
+        gained = [new([P, S], F32, "gained%d" % t) for t in range(PACK)]
+        for t in range(PACK):
+            nc.scalar.activation(size[t][:], h_bank[t][:], ACT.Abs)
+            nc.sync.dma_start(size_again[t][:], size[t][:])
+        for t in range(PACK):
+            if t < GAINS_ON_VECTOR:
+                nc.vector.tensor_scalar(gained[t][:], h_bank[t][:], gn_sb[:, t : t + 1], None, ALU.mult)
+            else:
+                nc.scalar.activation(gained[t][:], h_bank[t][:], ACT.Copy, scale=gn_sb[:, t : t + 1])
+        deal(nc.vector.tensor_copy, w_dealt_s[:], w_plain_s[:])
+
+        last = len(Z_CHUNKS) - 1
+        last_c0, last_n = Z_CHUNKS[last]
+        early_bank = [psum.tile([P, last_c0], F32, name="early_bank%d" % t) for t in range(PACK)]
+        last_bank = psum.tile([P, PACK, last_n], F32, name="last_bank", tag="bank0")
+
+        def h2_sums(c, t):
+            c0, n = Z_CHUNKS[c]
+            return last_bank[:, t, :] if c == last else early_bank[t][:, c0 : c0 + n]
+
+        for c, (c0, n) in enumerate(Z_CHUNKS):
+            for t in range(PACK):
+                cols = slice(t * P, (t + 1) * P)
+                nc.tensor.matmul_mx(
+                    out=h2_sums(c, t), lhsT=w2_dealt[:, cols].bitcast(FP8X4), lhsT_scale=w_dealt_s[4:P, cols],
+                    rhs=x2_w[:, c0 : c0 + n].bitcast(FP8X4), rhs_scale=x2_s[:, c0 : c0 + n],
+                    start=(c == 0 or (c == last and t == 0)), stop=False,
+                )
+
+        work = []
+        for c, (c0, n) in enumerate(Z_CHUNKS):
+            work.append({name: new([P, PACK, n], F32, "%s%d" % (name, c)) for name in ("den", "root", "factor", "top")})
+
+        def interleave(c):
+            c0, n = Z_CHUNKS[c]
+            factor = work[c]["root" if c == VECTOR_CHUNK else "factor"]
+            z_bf = new([P, n, PACK], BF16, "z_bf%d" % c)
+            walk = "p t (c i) -> p c t i"
+            nc.vector.tensor_tensor(
+                z_bf[:].rearrange("p (c i) t -> p c t i", i=4),
+                work[c]["top"][:].rearrange(walk, i=4), factor[:].rearrange(walk, i=4), ALU.mult,
+            )
+            return z_bf
+
+        def second_product(c, z_bf):
+            c0, n = Z_CHUNKS[c]
+            z_w = new([P, n], U32, "z_w%d" % c)
+            z_s = new([P, n], U8, "z_s%d" % c)
+            nc.vector.quantize_mx(out=z_w[:].bitcast(FP8X4), scales=z_s[:], in_=z_bf[:].rearrange("p c t -> p (c t)"))
+            for t in range(PACK):
+                cols = slice(t * P, (t + 1) * P)
+                nc.tensor.matmul_mx(
+                    out=h2_sums(c, t), lhsT=w1_dealt[:, cols].bitcast(FP8X4), lhsT_scale=w_dealt_s[:, cols],
+                    rhs=z_w[:].bitcast(FP8X4), rhs_scale=z_s[:],
+                    start=False, stop=(c == last - 1 or (c == last and t == PACK - 1)),
+                )
+
+        for c, (c0, n) in enumerate(Z_CHUNKS):
+            if c != VECTOR_CHUNK:
+                for t in range(PACK):
+                    nc.scalar.activation(work[c]["top"][:, t, :], gained[t][:].indirect(entries(lists["n1"], c0, n)), ACT.Copy)
+            for t in range(PACK):
+                nc.vector.tensor_tensor(
+                    work[c]["den"][:, t, :], size[t][:].indirect(entries(lists["n2"], c0, n)),
+                    size_again[t][:, c0 : c0 + n], ALU.add,
+                )
+            if c > 0:
+                z_bf = interleave(c - 1)
+            for pair in (slice(0, 2), slice(2, 4)):
+                nc.scalar.activation(work[c]["root"][:, pair, :], work[c]["den"][:, pair, :], ACT.Abs_reciprocal_sqrt, bias=8.0)
+                if c != VECTOR_CHUNK:
+                    nc.scalar.activation(work[c]["factor"][:, pair, :], work[c]["root"][:, pair, :], ACT.Square)
+            if c > 0:
+                second_product(c - 1, z_bf)
+            if c == VECTOR_CHUNK:
+                for t in range(PACK):
+                    nc.vector.tensor_tensor(
+                        work[c]["top"][:, t, :], gained[t][:].indirect(entries(lists["n1"], c0, n)),
+                        work[c]["root"][:, t, :], ALU.mult,
+                    )
+
+        h2 = [new([P, S], F32, "h2_%d" % t) for t in range(PACK)]
+        second_product(last, interleave(last))
+        for t in range(PACK):
+            nc.vector.tensor_copy(h2[t][:, :last_c0], early_bank[t][:])
+            nc.vector.tensor_copy(h2[t][:, last_c0:], last_bank[:, t, :])
+        y_s = new([P, S], U8, "y_s")
+        out_rows = out_0.rearrange("(p t) j -> p t j", t=PACK)
+        out_words = words_view(out_1)
+        for c, (c0, n) in enumerate(Y_CHUNKS):
+            sg = new([P, PACK, n], F32, "sg%d" % c)
+            sg2 = new([P, PACK, n], F32, "sg2_%d" % c)
+            diff = new([P, PACK, n], F32, "diff%d" % c)
+            y = new([P, PACK, n], F32, "y%d" % c)
+            y_bf = new([P, n, PACK], BF16, "y_bf%d" % c)
+            y_w = new([P, n], U32, "y_w%d" % c)
+            group = 1 if c == len(Y_CHUNKS) - 1 else 2
+            for t0 in range(0, PACK, group):
+                for t in range(t0, t0 + group):
+                    scale = sl_sb[:, t : t + 1]
+                    picked = h2[t][:].indirect(entries(lists["n3"], c0, n))
+                    nc.scalar.activation(sg[:, t, :], picked, ACT.Sigmoid, bias=bias_lo[:, t : t + 1], scale=scale)
+                    nc.scalar.activation(sg2[:, t, :], picked, ACT.Sigmoid, bias=bias_hi[:, t : t + 1], scale=scale)
+                ts = slice(t0, t0 + group)
+                nc.vector.tensor_tensor(diff[:, ts, :], sg[:, ts, :], sg2[:, ts, :], ALU.subtract)
+                for t in range(t0, t0 + group):
+                    nc.vector.tensor_tensor(y[:, t, :], diff[:, t, :], h2[t][:, c0 : c0 + n], ALU.mult)
+            nc.sync.dma_start(out_rows[:, :, c0 : c0 + n], y[:])
+            nc.vector.tensor_copy(
+                y_bf[:].rearrange("p (c i) t -> p c t i", i=4), y[:].rearrange("p t (c i) -> p c t i", i=4)
+            )
+            nc.vector.quantize_mx(
+                out=y_w[:].bitcast(FP8X4), scales=y_s[:, c0 : c0 + n], in_=y_bf[:].rearrange("p c t -> p (c t)")
+            )
+            nc.sync.dma_start(out_words[:, c0 : c0 + n], y_w[:].bitcast(I32))
+        for r in range(4):
+            queue = (nc.scalar, nc.sync)[r % 2]
+            queue.dma_start(out_2[0][r:16:4, :].bitcast(I32), y_s[r:P:32, :].bitcast(I32))

@@ -86,6 +86,8 @@ def tile_picked_pqmixnorm2ebd_none_po_kernel(
         w2_plain, w1_plain = w_plain[:, :N], w_plain[:, N:]
         nc.sync.dma_start(w2_plain.bitcast(I32), words_view(w2_words))
         nc.sync.dma_start(w1_plain.bitcast(I32), words_view(w1_words))
+        warm = new([P, 16], F32, "warm")
+        nc.scalar.activation(warm[:, 8:9], gn_sb[:, 0:1], ACT.Abs_reciprocal_sqrt, bias=1.0, scale=0.0)
         d_pick_w = keep.tile([P, H], U32, name="d_pick_w", tag="d_pick", align_bytes=64)
         nc.vector.tensor_copy(d_pick_w[:], d_table_w[:].indirect(lists["k1"][:]))
         nc.vector.tensor_copy(xq_w[:], x_table_w[:].indirect(lists["offs"][:]))
@@ -206,6 +208,7 @@ def tile_picked_pqmixnorm2ebd_none_po_kernel(
                         work[c]["root"][:, t, :], ALU.mult,
                     )
 
+        nc.scalar.activation(warm[:, 9:10], work[last]["factor"][:, PACK - 1, last_n - 1 :], ACT.Sigmoid)
         h2 = [new([P, S], F32, "h2_%d" % t) for t in range(PACK)]
         second_product(last, interleave(last))
         for t in range(PACK):

@@ -20,6 +20,7 @@ PACK = 4
 Z_CHUNKS = ((0, 256), (256, 128), (384, 128))
 VECTOR_CHUNK = 1
 GAINS_ON_VECTOR = 2
+EARLY_ON_SCALAR = 2
 Y_CHUNKS = ((0, 256), (256, 128), (384, 128))
 
 
@@ -62,8 +63,8 @@ def tile_picked_pqmixnorm2ebd_none_po_kernel(
         nc.sync.dma_start(lists["k1"][:], k1)
         nc.sync.dma_start(d_table_s[:].bitcast(I32), d_scales[0].bitcast(I32).unsqueeze(1).to_broadcast([16, 8, G // 4]))
         nc.sync.dma_start(lists["offs"][:], offs)
-        nc.sync.dma_start(d_table_w[:].bitcast(I32), words_view(d_words))
         nc.sync.dma_start(x_table_w[:].bitcast(I32), words_view(x_words))
+        nc.sync.dma_start(d_table_w[:].bitcast(I32), words_view(d_words))
         for r in range(4):
             nc.scalar.dma_start(x_table_s[r:P:32, :].bitcast(I32), x_scales[0][r:16:4, :].bitcast(I32))
         nc.sync.dma_start(lists["two"][:], two)
@@ -76,12 +77,12 @@ def tile_picked_pqmixnorm2ebd_none_po_kernel(
         d_dealt_s = new([P, H], U8, "d_dealt_s")
         d_dealt_w = new([P, H], U32, "d_dealt_w")
         xq_w = new([P, S], U32, "xq_w")
-        xq_s = new([P, S], U8, "xq_s")
+        xq_s = keep.tile([P, S], U8, name="xq_s", tag="x_pick_s", align_bytes=64)
         nc.vector.tensor_copy(d_pick_s[:], d_table_s[:].indirect(lists["k1"][:]))
+        nc.vector.tensor_copy(xq_w[:], x_table_w[:].indirect(lists["offs"][:]))
         deal(nc.vector.tensor_copy, d_dealt_s[:], d_pick_s[:])
         for r in range(1, 4):
-            queue = (nc.sync, nc.scalar)[r % 2]
-            queue.dma_start(d_dealt_s[r:P:32, :].bitcast(I32), d_dealt_s[8 * r : P : 32, :].bitcast(I32))
+            nc.scalar.dma_start(d_dealt_s[r:P:32, :].bitcast(I32), d_dealt_s[8 * r : P : 32, :].bitcast(I32))
         w_plain = keep.tile([P, 2 * N], U32, name="w_plain", tag="d_scales_then_w", align_bytes=64)
         w2_plain, w1_plain = w_plain[:, :N], w_plain[:, N:]
         nc.sync.dma_start(w2_plain.bitcast(I32), words_view(w2_words))
@@ -89,10 +90,9 @@ def tile_picked_pqmixnorm2ebd_none_po_kernel(
         warm = new([P, 16], F32, "warm")
         nc.scalar.activation(warm[:, 8:9], gn_sb[:, 0:1], ACT.Abs_reciprocal_sqrt, bias=1.0, scale=0.0)
         d_pick_w = keep.tile([P, H], U32, name="d_pick_w", tag="d_pick", align_bytes=64)
-        nc.vector.tensor_copy(d_pick_w[:], d_table_w[:].indirect(lists["k1"][:]))
-        nc.vector.tensor_copy(xq_w[:], x_table_w[:].indirect(lists["offs"][:]))
-        deal(nc.vector.tensor_copy, d_dealt_w[:], d_pick_w[:])
         nc.vector.tensor_copy(xq_s[:], x_table_s[:].indirect(lists["offs"][:]))
+        nc.vector.tensor_copy(d_pick_w[:], d_table_w[:].indirect(lists["k1"][:]))
+        deal(nc.vector.tensor_copy, d_dealt_w[:], d_pick_w[:])
 
         w_plain_s = keep.tile([P, N], U8, name="w_plain_s", tag="d_then_w", align_bytes=64)
         nc.gpsimd.memset(w_plain_s[:].bitcast(I32), 0)
@@ -114,8 +114,8 @@ def tile_picked_pqmixnorm2ebd_none_po_kernel(
                 rhs=xq_w[:].bitcast(FP8X4), rhs_scale=xq_s[:], start=True, stop=True,
             )
 
-        x2_w = new([P, S], U32, "x2_w")
-        x2_s = new([P, S], U8, "x2_s")
+        x2_w = keep.tile([P, S], U32, name="x2_w", tag="d_pick", align_bytes=64)
+        x2_s = keep.tile([P, S], U8, name="x2_s", tag="x_pick_s", align_bytes=64)
         nc.vector.tensor_copy(x2_w[:], x_table_w[:].indirect(lists["two"][:]))
         nc.vector.tensor_copy(x2_s[:], x_table_s[:].indirect(lists["two"][:]))
         minus_sl = new([P, PACK], F32, "minus_sl")
@@ -126,11 +126,14 @@ def tile_picked_pqmixnorm2ebd_none_po_kernel(
         nc.gpsimd.tensor_tensor(bias_hi[:], minus_sl[:], hi_sb[:], ALU.mult)
 
         size = [new([P, S], F32, "size%d" % t) for t in range(PACK)]
-        size_again = [new([P, S], F32, "size_again%d" % t) for t in range(PACK)]
+        half = S // 2
+        size_low = keep.tile([P, PACK, half], F32, name="size_low", tag="low_then_den", align_bytes=64)
+        size_high = new([P, PACK, half], F32, "size_high")
         gained = [new([P, S], F32, "gained%d" % t) for t in range(PACK)]
         for t in range(PACK):
             nc.scalar.activation(size[t][:], h_bank[t][:], ACT.Abs)
-            nc.sync.dma_start(size_again[t][:], size[t][:])
+            nc.sync.dma_start(size_low[:, t, :], size[t][:, :half])
+            nc.sync.dma_start(size_high[:, t, :], size[t][:, half:])
         for t in range(PACK):
             if t < GAINS_ON_VECTOR:
                 nc.vector.tensor_scalar(gained[t][:], h_bank[t][:], gn_sb[:, t : t + 1], None, ALU.mult)
@@ -158,7 +161,8 @@ def tile_picked_pqmixnorm2ebd_none_po_kernel(
 
         work = []
         for c, (c0, n) in enumerate(Z_CHUNKS):
-            work.append({name: new([P, PACK, n], F32, "%s%d" % (name, c)) for name in ("den", "root", "factor", "top")})
+            work.append({name: new([P, PACK, n], F32, "%s%d" % (name, c)) for name in ("root", "factor")})
+        den_low = keep.tile([P, PACK, half], F32, name="den_low", tag="den_then_top", align_bytes=64)
 
         def interleave(c):
             c0, n = Z_CHUNKS[c]
@@ -185,18 +189,25 @@ def tile_picked_pqmixnorm2ebd_none_po_kernel(
                 )
 
         for c, (c0, n) in enumerate(Z_CHUNKS):
+            if c == 1:
+                den_high = keep.tile([P, PACK, half], F32, name="den_high", tag="low_then_den", align_bytes=64)
+            if c == last:
+                work[c]["top"] = keep.tile([P, PACK, n], F32, name="top_last", tag="den_then_top", align_bytes=64)
+            else:
+                work[c]["top"] = new([P, PACK, n], F32, "top%d" % c)
+            own_size = size_low[:] if c == 0 else size_high[:, :, c0 - half : c0 - half + n]
+            den = den_low[:] if c == 0 else den_high[:, :, c0 - half : c0 - half + n]
             if c != VECTOR_CHUNK:
                 for t in range(PACK):
                     nc.scalar.activation(work[c]["top"][:, t, :], gained[t][:].indirect(entries(lists["n1"], c0, n)), ACT.Copy)
             for t in range(PACK):
                 nc.vector.tensor_tensor(
-                    work[c]["den"][:, t, :], size[t][:].indirect(entries(lists["n2"], c0, n)),
-                    size_again[t][:, c0 : c0 + n], ALU.add,
+                    den[:, t, :], size[t][:].indirect(entries(lists["n2"], c0, n)), own_size[:, t, :], ALU.add
                 )
             if c > 0:
                 z_bf = interleave(c - 1)
             for pair in (slice(0, 2), slice(2, 4)):
-                nc.scalar.activation(work[c]["root"][:, pair, :], work[c]["den"][:, pair, :], ACT.Abs_reciprocal_sqrt, bias=8.0)
+                nc.scalar.activation(work[c]["root"][:, pair, :], den[:, pair, :], ACT.Abs_reciprocal_sqrt, bias=8.0)
                 if c != VECTOR_CHUNK:
                     nc.scalar.activation(work[c]["factor"][:, pair, :], work[c]["root"][:, pair, :], ACT.Square)
             if c > 0:
@@ -212,7 +223,7 @@ def tile_picked_pqmixnorm2ebd_none_po_kernel(
         h2 = [new([P, S], F32, "h2_%d" % t) for t in range(PACK)]
         second_product(last, interleave(last))
         for t in range(PACK):
-            nc.vector.tensor_copy(h2[t][:, :last_c0], early_bank[t][:])
+            (nc.scalar.copy if t < EARLY_ON_SCALAR else nc.vector.tensor_copy)(h2[t][:, :last_c0], early_bank[t][:])
             nc.vector.tensor_copy(h2[t][:, last_c0:], last_bank[:, t, :])
         y_s = new([P, S], U8, "y_s")
         out_rows = out_0.rearrange("(p t) j -> p t j", t=PACK)
@@ -224,7 +235,7 @@ def tile_picked_pqmixnorm2ebd_none_po_kernel(
             y = new([P, PACK, n], F32, "y%d" % c)
             y_bf = new([P, n, PACK], BF16, "y_bf%d" % c)
             y_w = new([P, n], U32, "y_w%d" % c)
-            group = 1 if c == len(Y_CHUNKS) - 1 else 2
+            group = 1
             for t0 in range(0, PACK, group):
                 for t in range(t0, t0 + group):
                     scale = sl_sb[:, t : t + 1]
@@ -235,7 +246,10 @@ def tile_picked_pqmixnorm2ebd_none_po_kernel(
                 nc.vector.tensor_tensor(diff[:, ts, :], sg[:, ts, :], sg2[:, ts, :], ALU.subtract)
                 for t in range(t0, t0 + group):
                     nc.vector.tensor_tensor(y[:, t, :], diff[:, t, :], h2[t][:, c0 : c0 + n], ALU.mult)
-            nc.sync.dma_start(out_rows[:, :, c0 : c0 + n], y[:])
+                    if c == len(Y_CHUNKS) - 1:
+                        nc.sync.dma_start(out_rows[:, t, c0 : c0 + n], y[:, t, :])
+            if c < len(Y_CHUNKS) - 1:
+                nc.sync.dma_start(out_rows[:, :, c0 : c0 + n], y[:])
             nc.vector.tensor_copy(
                 y_bf[:].rearrange("p (c i) t -> p c t i", i=4), y[:].rearrange("p t (c i) -> p c t i", i=4)
             )

@@ -49,8 +49,10 @@ def tile_picked_pqmixnorm2ebd_none_po_kernel(
             return keep.tile(shape, dtype, name=name, align_bytes=64)
 
         lists = {name: new([P, 32], U16, "list_" + name) for name in ("k1", "offs", "two", "n2", "n1", "n3")}
-        d_table_w = keep.tile([P, G], U32, name="d_table_w", tag="d_then_w", align_bytes=64)
-        d_table_s = keep.tile([P, G], U8, name="d_table_s", tag="d_scales_then_w", align_bytes=64)
+        d_table_w = new([P, G], U32, "d_table_w")
+        d_table_s = new([P, G], U8, "d_table_s")
+        w1_plain = new([P, N], U32, "w1_plain")
+        w2_plain = new([P, N], U32, "w2_plain")
         x_table_w = new([P, T], U32, "x_table_w")
         x_table_s = new([P, T], U8, "x_table_s")
         gn_sb = new([P, PACK], F32, "gn_sb")
@@ -58,7 +60,9 @@ def tile_picked_pqmixnorm2ebd_none_po_kernel(
         lo_sb = new([P, PACK], F32, "lo_sb")
         hi_sb = new([P, PACK], F32, "hi_sb")
 
+        w_plain_s = new([P, N], U8, "w_plain_s")
         nc.vector.memset(x_table_s[:].bitcast(I32), 0)
+        nc.gpsimd.memset(w_plain_s[:].bitcast(I32), 0)
 
         nc.sync.dma_start(lists["k1"][:], k1)
         nc.sync.dma_start(d_table_s[:].bitcast(I32), d_scales[0].bitcast(I32).unsqueeze(1).to_broadcast([16, 8, G // 4]))
@@ -68,12 +72,17 @@ def tile_picked_pqmixnorm2ebd_none_po_kernel(
         for r in range(4):
             nc.scalar.dma_start(x_table_s[r:P:32, :].bitcast(I32), x_scales[0][r:16:4, :].bitcast(I32))
         nc.sync.dma_start(lists["two"][:], two)
+        nc.sync.dma_start(w2_plain[:].bitcast(I32), words_view(w2_words))
+        nc.sync.dma_start(w1_plain[:].bitcast(I32), words_view(w1_words))
         for name, src in (("n2", n2), ("n1", n1), ("n3", n3)):
             nc.sync.dma_start(lists[name][:], src)
+        for first_row, scales in ((4, w2_scales), (0, w1_scales)):
+            for r in range(4):
+                nc.sync.dma_start(w_plain_s[first_row + r : P : 32, :].bitcast(I32), scales[0][r:16:4, :].bitcast(I32))
         for tile, src in ((gn_sb, gn), (sl_sb, sl), (lo_sb, lo), (hi_sb, hi)):
             nc.gpsimd.dma_start(tile[:], src.rearrange("(p t) o -> p (t o)", t=PACK))
 
-        d_pick_s = keep.tile([P, H], U8, name="d_pick_s", tag="d_pick", align_bytes=64)
+        d_pick_s = new([P, H], U8, "d_pick_s")
         d_dealt_s = new([P, H], U8, "d_dealt_s")
         d_dealt_w = new([P, H], U32, "d_dealt_w")
         xq_w = new([P, S], U32, "xq_w")
@@ -83,10 +92,6 @@ def tile_picked_pqmixnorm2ebd_none_po_kernel(
         deal(nc.vector.tensor_copy, d_dealt_s[:], d_pick_s[:])
         for r in range(1, 4):
             nc.scalar.dma_start(d_dealt_s[r:P:32, :].bitcast(I32), d_dealt_s[8 * r : P : 32, :].bitcast(I32))
-        w_plain = keep.tile([P, 2 * N], U32, name="w_plain", tag="d_scales_then_w", align_bytes=64)
-        w2_plain, w1_plain = w_plain[:, :N], w_plain[:, N:]
-        nc.sync.dma_start(w2_plain.bitcast(I32), words_view(w2_words))
-        nc.sync.dma_start(w1_plain.bitcast(I32), words_view(w1_words))
         warm = new([P, 16], F32, "warm")
         nc.scalar.activation(warm[:, 8:9], gn_sb[:, 0:1], ACT.Abs_reciprocal_sqrt, bias=1.0, scale=0.0)
         d_pick_w = keep.tile([P, H], U32, name="d_pick_w", tag="d_pick", align_bytes=64)
@@ -94,17 +99,11 @@ def tile_picked_pqmixnorm2ebd_none_po_kernel(
         nc.vector.tensor_copy(d_pick_w[:], d_table_w[:].indirect(lists["k1"][:]))
         deal(nc.vector.tensor_copy, d_dealt_w[:], d_pick_w[:])
 
-        w_plain_s = keep.tile([P, N], U8, name="w_plain_s", tag="d_then_w", align_bytes=64)
-        nc.gpsimd.memset(w_plain_s[:].bitcast(I32), 0)
-        for first_row, scales in ((4, w2_scales), (0, w1_scales)):
-            for r in range(4):
-                nc.sync.dma_start(w_plain_s[first_row + r : P : 32, :].bitcast(I32), scales[0][r:16:4, :].bitcast(I32))
-
         w1_dealt = new([P, N], U32, "w1_dealt")
         w2_dealt = new([P, N], U32, "w2_dealt")
         w_dealt_s = new([P, N], U8, "w_dealt_s")
-        deal(nc.scalar.copy, w2_dealt[:], w2_plain)
-        deal(nc.scalar.copy, w1_dealt[:], w1_plain)
+        deal(nc.scalar.copy, w2_dealt[:], w2_plain[:])
+        deal(nc.scalar.copy, w1_dealt[:], w1_plain[:])
 
         h_bank = [psum.tile([P, S], F32, name="h_bank%d" % t, tag="bank%d" % t) for t in range(PACK)]
         for t in range(PACK):
@@ -127,13 +126,14 @@ def tile_picked_pqmixnorm2ebd_none_po_kernel(
 
         size = [new([P, S], F32, "size%d" % t) for t in range(PACK)]
         half = S // 2
-        size_low = keep.tile([P, PACK, half], F32, name="size_low", tag="low_then_den", align_bytes=64)
-        size_high = new([P, PACK, half], F32, "size_high")
+        size_low = [new([P, half], F32, "size_low%d" % t) for t in range(PACK - 1)]
+        size_low.append(keep.tile([P, half], F32, name="size_low3", tag="low_then_den", align_bytes=64))
+        size_high = [new([P, half], F32, "size_high%d" % t) for t in range(PACK)]
         gained = [new([P, S], F32, "gained%d" % t) for t in range(PACK)]
         for t in range(PACK):
             nc.scalar.activation(size[t][:], h_bank[t][:], ACT.Abs)
-            nc.sync.dma_start(size_low[:, t, :], size[t][:, :half])
-            nc.sync.dma_start(size_high[:, t, :], size[t][:, half:])
+            nc.sync.dma_start(size_low[t][:], size[t][:, :half])
+            nc.sync.dma_start(size_high[t][:], size[t][:, half:])
         for t in range(PACK):
             if t < GAINS_ON_VECTOR:
                 nc.vector.tensor_scalar(gained[t][:], h_bank[t][:], gn_sb[:, t : t + 1], None, ALU.mult)
@@ -188,38 +188,45 @@ def tile_picked_pqmixnorm2ebd_none_po_kernel(
                     start=False, stop=(c == last - 1 or (c == last and t == PACK - 1)),
                 )
 
-        for c, (c0, n) in enumerate(Z_CHUNKS):
-            if c == 1:
-                den_high = keep.tile([P, PACK, half], F32, name="den_high", tag="low_then_den", align_bytes=64)
-            if c == last:
-                work[c]["top"] = keep.tile([P, PACK, n], F32, name="top_last", tag="den_then_top", align_bytes=64)
-            else:
-                work[c]["top"] = new([P, PACK, n], F32, "top%d" % c)
-            own_size = size_low[:] if c == 0 else size_high[:, :, c0 - half : c0 - half + n]
-            den = den_low[:] if c == 0 else den_high[:, :, c0 - half : c0 - half + n]
-            if c != VECTOR_CHUNK:
-                for t in range(PACK):
-                    nc.scalar.activation(work[c]["top"][:, t, :], gained[t][:].indirect(entries(lists["n1"], c0, n)), ACT.Copy)
+        def fetch_top(c):
+            c0, n = Z_CHUNKS[c]
             for t in range(PACK):
-                nc.vector.tensor_tensor(
-                    den[:, t, :], size[t][:].indirect(entries(lists["n2"], c0, n)), own_size[:, t, :], ALU.add
-                )
-            if c > 0:
-                z_bf = interleave(c - 1)
+                picked = gained[t][:].indirect(entries(lists["n1"], c0, n))
+                if c == VECTOR_CHUNK:
+                    nc.vector.tensor_tensor(work[c]["top"][:, t, :], picked, work[c]["root"][:, t, :], ALU.mult)
+                else:
+                    nc.scalar.activation(work[c]["top"][:, t, :], picked, ACT.Copy)
+
+        def denominators(c, den, own_size):
+            c0, n = Z_CHUNKS[c]
+            for t in range(PACK):
+                nc.vector.tensor_tensor(den[:, t, :], size[t][:].indirect(entries(lists["n2"], c0, n)), own_size[t], ALU.add)
+
+        def roots(c, den):
             for pair in (slice(0, 2), slice(2, 4)):
                 nc.scalar.activation(work[c]["root"][:, pair, :], den[:, pair, :], ACT.Abs_reciprocal_sqrt, bias=8.0)
                 if c != VECTOR_CHUNK:
                     nc.scalar.activation(work[c]["factor"][:, pair, :], work[c]["root"][:, pair, :], ACT.Square)
-            if c > 0:
-                second_product(c - 1, z_bf)
-            if c == VECTOR_CHUNK:
-                for t in range(PACK):
-                    nc.vector.tensor_tensor(
-                        work[c]["top"][:, t, :], gained[t][:].indirect(entries(lists["n1"], c0, n)),
-                        work[c]["root"][:, t, :], ALU.mult,
-                    )
 
-        nc.scalar.activation(warm[:, 9:10], work[last]["factor"][:, PACK - 1, last_n - 1 :], ACT.Sigmoid)
+        work[0]["top"] = new([P, PACK, half], F32, "top0")
+        work[1]["top"] = new([P, PACK, half // 2], F32, "top1")
+        fetch_top(0)
+        denominators(0, den_low[:], [tile[:] for tile in size_low])
+        den_high = keep.tile([P, 2, PACK, half // 2], F32, name="den_high", tag="low_then_den", align_bytes=64)
+        den = [den_low[:], den_high[:, 0, :, :], den_high[:, 1, :, :]]
+        denominators(1, den[1], [tile[:, : half // 2] for tile in size_high])
+        denominators(2, den[2], [tile[:, half // 2 :] for tile in size_high])
+        roots(0, den[0])
+        roots(1, den[1])
+        work[2]["top"] = keep.tile([P, PACK, half // 2], F32, name="top_last", tag="den_then_top", align_bytes=64)
+        fetch_top(2)
+        roots(2, den[2])
+        z_bf = interleave(0)
+        fetch_top(1)
+        second_product(0, z_bf)
+        second_product(1, interleave(1))
+
+        nc.scalar.activation(warm[:, 9:10], work[last]["root"][:, PACK - 1, last_n - 1 :], ACT.Sigmoid)
         h2 = [new([P, S], F32, "h2_%d" % t) for t in range(PACK)]
         second_product(last, interleave(last))
         for t in range(PACK):

@@ -49,7 +49,7 @@ def tile_picked_pqmixnorm2ebd_none_po_kernel(
             return keep.tile(shape, dtype, name=name, align_bytes=64)
 
         lists = {name: new([P, 32], U16, "list_" + name) for name in ("k1", "offs", "two", "n2", "n1", "n3")}
-        d_table_w = new([P, G], U32, "d_table_w")
+        d_table_w = keep.tile([P, G], U32, name="d_table_w", tag="x_pick_s", align_bytes=64)
         d_table_s = new([P, G], U8, "d_table_s")
         w1_plain = new([P, N], U32, "w1_plain")
         w2_plain = new([P, N], U32, "w2_plain")
@@ -86,7 +86,6 @@ def tile_picked_pqmixnorm2ebd_none_po_kernel(
         d_dealt_s = new([P, H], U8, "d_dealt_s")
         d_dealt_w = new([P, H], U32, "d_dealt_w")
         xq_w = new([P, S], U32, "xq_w")
-        xq_s = keep.tile([P, S], U8, name="xq_s", tag="x_pick_s", align_bytes=64)
         nc.vector.tensor_copy(d_pick_s[:], d_table_s[:].indirect(lists["k1"][:]))
         nc.vector.tensor_copy(xq_w[:], x_table_w[:].indirect(lists["offs"][:]))
         deal(nc.vector.tensor_copy, d_dealt_s[:], d_pick_s[:])
@@ -95,8 +94,9 @@ def tile_picked_pqmixnorm2ebd_none_po_kernel(
         warm = new([P, 16], F32, "warm")
         nc.scalar.activation(warm[:, 8:9], gn_sb[:, 0:1], ACT.Abs_reciprocal_sqrt, bias=1.0, scale=0.0)
         d_pick_w = keep.tile([P, H], U32, name="d_pick_w", tag="d_pick", align_bytes=64)
-        nc.vector.tensor_copy(xq_s[:], x_table_s[:].indirect(lists["offs"][:]))
         nc.vector.tensor_copy(d_pick_w[:], d_table_w[:].indirect(lists["k1"][:]))
+        xq_s = keep.tile([P, S], U8, name="xq_s", tag="x_pick_s", align_bytes=64)
+        nc.vector.tensor_copy(xq_s[:], x_table_s[:].indirect(lists["offs"][:]))
         deal(nc.vector.tensor_copy, d_dealt_w[:], d_pick_w[:])
 
         w1_dealt = new([P, N], U32, "w1_dealt")
@@ -144,11 +144,11 @@ def tile_picked_pqmixnorm2ebd_none_po_kernel(
         last = len(Z_CHUNKS) - 1
         last_c0, last_n = Z_CHUNKS[last]
         early_bank = [psum.tile([P, last_c0], F32, name="early_bank%d" % t) for t in range(PACK)]
-        last_bank = psum.tile([P, PACK, last_n], F32, name="last_bank", tag="bank0")
+        last_bank = [psum.tile([P, last_n], F32, name="last_bank%d" % t, tag="bank%d" % t) for t in range(PACK)]
 
         def h2_sums(c, t):
             c0, n = Z_CHUNKS[c]
-            return last_bank[:, t, :] if c == last else early_bank[t][:, c0 : c0 + n]
+            return last_bank[t][:] if c == last else early_bank[t][:, c0 : c0 + n]
 
         for c, (c0, n) in enumerate(Z_CHUNKS):
             for t in range(PACK):
@@ -156,7 +156,7 @@ def tile_picked_pqmixnorm2ebd_none_po_kernel(
                 nc.tensor.matmul_mx(
                     out=h2_sums(c, t), lhsT=w2_dealt[:, cols].bitcast(FP8X4), lhsT_scale=w_dealt_s[4:P, cols],
                     rhs=x2_w[:, c0 : c0 + n].bitcast(FP8X4), rhs_scale=x2_s[:, c0 : c0 + n],
-                    start=(c == 0 or (c == last and t == 0)), stop=False,
+                    start=(c == 0 or c == last), stop=False,
                 )
 
         work = []
@@ -185,7 +185,7 @@ def tile_picked_pqmixnorm2ebd_none_po_kernel(
                 nc.tensor.matmul_mx(
                     out=h2_sums(c, t), lhsT=w1_dealt[:, cols].bitcast(FP8X4), lhsT_scale=w_dealt_s[:, cols],
                     rhs=z_w[:].bitcast(FP8X4), rhs_scale=z_s[:],
-                    start=False, stop=(c == last - 1 or (c == last and t == PACK - 1)),
+                    start=False, stop=(c >= last - 1),
                 )
 
         def fetch_top(c):
@@ -231,7 +231,7 @@ def tile_picked_pqmixnorm2ebd_none_po_kernel(
         second_product(last, interleave(last))
         for t in range(PACK):
             (nc.scalar.copy if t < EARLY_ON_SCALAR else nc.vector.tensor_copy)(h2[t][:, :last_c0], early_bank[t][:])
-            nc.vector.tensor_copy(h2[t][:, last_c0:], last_bank[:, t, :])
+            nc.vector.tensor_copy(h2[t][:, last_c0:], last_bank[t][:])
         y_s = new([P, S], U8, "y_s")
         out_rows = out_0.rearrange("(p t) j -> p t j", t=PACK)
         out_words = words_view(out_1)

from contextlib import ExitStack

import concourse.mybir as mybir

K, T, S, N, G, H = 512, 1024, 512, 512, 2048, 512
FLOPS = 3 * 2 * 512 * 512 * 512

F32 = mybir.dt.float32
BF16 = mybir.dt.bfloat16
I32 = mybir.dt.int32
U32 = mybir.dt.uint32
U16 = mybir.dt.uint16
U8 = mybir.dt.uint8
FP8X4 = mybir.dt.float8_e4m3fn_x4
ALU = mybir.AluOpType
ACT = mybir.ActivationFunctionType

P = 128
PACK = 4
Z_CHUNKS = ((0, 256), (256, 128), (384, 128))
VECTOR_CHUNK = 1
GAINS_ON_VECTOR = 2
EARLY_ON_SCALAR = 2
Y_CHUNKS = ((0, 256), (256, 128), (384, 128))


def words_view(dram):
    return dram[0].rearrange("p n t -> p (n t)").bitcast(I32)


def entries(offsets, start, count):
    return offsets[:, start // 16 : (start + count) // 16]


def deal(engine_copy, dealt, plain):
    engine_copy(dealt.rearrange("p (t m) -> p m t", t=PACK), plain.rearrange("p (m t) -> p m t", t=PACK))


def tile_picked_pqmixnorm2ebd_none_po_kernel(
    tc, x_words, x_scales, d_words, d_scales, gn, w1_words, w1_scales, w2_words, w2_scales, sl, lo, hi,
    offs, k1, n1, n2, two, n3, out_0, out_1, out_2,
):
    nc = tc.nc
    with ExitStack() as ctx:
        keep = ctx.enter_context(tc.tile_pool(name="keep", bufs=1))
        psum = ctx.enter_context(tc.psum_pool(name="psum", bufs=1))

        def new(shape, dtype, name):
            return keep.tile(shape, dtype, name=name, align_bytes=64)

        lists = {name: new([P, 32], U16, "list_" + name) for name in ("k1", "offs", "two", "n2", "n1", "n3")}
        d_table_w = keep.tile([P, G], U32, name="d_table_w", tag="x_pick_s", align_bytes=64)
        d_table_s = new([P, G], U8, "d_table_s")
        w1_plain = new([P, N], U32, "w1_plain")
        w2_plain = new([P, N], U32, "w2_plain")
        x_table_w = new([P, T], U32, "x_table_w")
        x_table_s = new([P, T], U8, "x_table_s")
        gn_sb = new([P, PACK], F32, "gn_sb")
        sl_sb = new([P, PACK], F32, "sl_sb")
        lo_sb = new([P, PACK], F32, "lo_sb")
        hi_sb = new([P, PACK], F32, "hi_sb")

        w_plain_s = new([P, N], U8, "w_plain_s")
        nc.vector.memset(x_table_s[:].bitcast(I32), 0)
        nc.gpsimd.memset(w_plain_s[:].bitcast(I32), 0)

        nc.sync.dma_start(lists["k1"][:], k1)
        nc.sync.dma_start(d_table_s[:].bitcast(I32), d_scales[0].bitcast(I32).unsqueeze(1).to_broadcast([16, 8, G // 4]))
        nc.sync.dma_start(lists["offs"][:], offs)
        nc.sync.dma_start(x_table_w[:].bitcast(I32), words_view(x_words))
        nc.sync.dma_start(d_table_w[:].bitcast(I32), words_view(d_words))
        for r in range(4):
            nc.scalar.dma_start(x_table_s[r:P:32, :].bitcast(I32), x_scales[0][r:16:4, :].bitcast(I32))
        nc.sync.dma_start(lists["two"][:], two)
        nc.sync.dma_start(w2_plain[:].bitcast(I32), words_view(w2_words))
        nc.sync.dma_start(w1_plain[:].bitcast(I32), words_view(w1_words))
        for name, src in (("n2", n2), ("n1", n1), ("n3", n3)):
            nc.sync.dma_start(lists[name][:], src)
        for first_row, scales in ((4, w2_scales), (0, w1_scales)):
            for r in range(4):
                nc.sync.dma_start(w_plain_s[first_row + r : P : 32, :].bitcast(I32), scales[0][r:16:4, :].bitcast(I32))
        for tile, src in ((gn_sb, gn), (sl_sb, sl), (lo_sb, lo), (hi_sb, hi)):
            nc.gpsimd.dma_start(tile[:], src.rearrange("(p t) o -> p (t o)", t=PACK))

        d_pick_s = new([P, H], U8, "d_pick_s")
        d_dealt_s = new([P, H], U8, "d_dealt_s")
        d_dealt_w = new([P, H], U32, "d_dealt_w")
        xq_w = new([P, S], U32, "xq_w")
        nc.vector.tensor_copy(d_pick_s[:], d_table_s[:].indirect(lists["k1"][:]))
        nc.vector.tensor_copy(xq_w[:], x_table_w[:].indirect(lists["offs"][:]))
        deal(nc.vector.tensor_copy, d_dealt_s[:], d_pick_s[:])
        for r in range(1, 4):
            nc.scalar.dma_start(d_dealt_s[r:P:32, :].bitcast(I32), d_dealt_s[8 * r : P : 32, :].bitcast(I32))
        warm = new([P, 16], F32, "warm")
        nc.scalar.activation(warm[:, 8:9], gn_sb[:, 0:1], ACT.Abs_reciprocal_sqrt, bias=1.0, scale=0.0)
        d_pick_w = keep.tile([P, H], U32, name="d_pick_w", tag="d_pick", align_bytes=64)
        nc.vector.tensor_copy(d_pick_w[:], d_table_w[:].indirect(lists["k1"][:]))
        xq_s = keep.tile([P, S], U8, name="xq_s", tag="x_pick_s", align_bytes=64)
        nc.vector.tensor_copy(xq_s[:], x_table_s[:].indirect(lists["offs"][:]))
        deal(nc.vector.tensor_copy, d_dealt_w[:], d_pick_w[:])

        w1_dealt = new([P, N], U32, "w1_dealt")
        w2_dealt = new([P, N], U32, "w2_dealt")
        w_dealt_s = new([P, N], U8, "w_dealt_s")
        deal(nc.scalar.copy, w2_dealt[:], w2_plain[:])
        deal(nc.scalar.copy, w1_dealt[:], w1_plain[:])

        h_bank = [psum.tile([P, S], F32, name="h_bank%d" % t, tag="bank%d" % t) for t in range(PACK)]
        for t in range(PACK):
            cols = slice(t * P, (t + 1) * P)
            nc.tensor.matmul_mx(
                out=h_bank[t][:], lhsT=d_dealt_w[:, cols].bitcast(FP8X4), lhsT_scale=d_dealt_s[:, cols],
                rhs=xq_w[:].bitcast(FP8X4), rhs_scale=xq_s[:], start=True, stop=True,
            )

        x2_w = keep.tile([P, S], U32, name="x2_w", tag="d_pick", align_bytes=64)
        x2_s = keep.tile([P, S], U8, name="x2_s", tag="x_pick_s", align_bytes=64)
        nc.vector.tensor_copy(x2_w[:], x_table_w[:].indirect(lists["two"][:]))
        nc.vector.tensor_copy(x2_s[:], x_table_s[:].indirect(lists["two"][:]))
        minus_sl = new([P, PACK], F32, "minus_sl")
        bias_lo = new([P, PACK], F32, "bias_lo")
        bias_hi = new([P, PACK], F32, "bias_hi")
        nc.gpsimd.tensor_scalar(minus_sl[:], sl_sb[:], -1.0, 0.0, ALU.mult, ALU.add)
        nc.gpsimd.tensor_tensor(bias_lo[:], minus_sl[:], lo_sb[:], ALU.mult)
        nc.gpsimd.tensor_tensor(bias_hi[:], minus_sl[:], hi_sb[:], ALU.mult)

        size = [new([P, S], F32, "size%d" % t) for t in range(PACK)]
        half = S // 2
        size_low = [new([P, half], F32, "size_low%d" % t) for t in range(PACK - 1)]
        size_low.append(keep.tile([P, half], F32, name="size_low3", tag="low_then_den", align_bytes=64))
        size_high = [new([P, half], F32, "size_high%d" % t) for t in range(PACK)]
        gained = [new([P, S], F32, "gained%d" % t) for t in range(PACK)]
        for t in range(PACK):
            nc.scalar.activation(size[t][:], h_bank[t][:], ACT.Abs)
            nc.sync.dma_start(size_low[t][:], size[t][:, :half])
            nc.sync.dma_start(size_high[t][:], size[t][:, half:])
        for t in range(PACK):
            if t < GAINS_ON_VECTOR:
                nc.vector.tensor_scalar(gained[t][:], h_bank[t][:], gn_sb[:, t : t + 1], None, ALU.mult)
            else:
                nc.scalar.activation(gained[t][:], h_bank[t][:], ACT.Copy, scale=gn_sb[:, t : t + 1])
        deal(nc.vector.tensor_copy, w_dealt_s[:], w_plain_s[:])

        last = len(Z_CHUNKS) - 1
        last_c0, last_n = Z_CHUNKS[last]
        early_bank = [psum.tile([P, last_c0], F32, name="early_bank%d" % t) for t in range(PACK)]
        last_bank = [psum.tile([P, last_n], F32, name="last_bank%d" % t, tag="bank%d" % t) for t in range(PACK)]

        def h2_sums(c, t):
            c0, n = Z_CHUNKS[c]
            return last_bank[t][:] if c == last else early_bank[t][:, c0 : c0 + n]

        for c, (c0, n) in enumerate(Z_CHUNKS):
            for t in range(PACK):
                cols = slice(t * P, (t + 1) * P)
                nc.tensor.matmul_mx(
                    out=h2_sums(c, t), lhsT=w2_dealt[:, cols].bitcast(FP8X4), lhsT_scale=w_dealt_s[4:P, cols],
                    rhs=x2_w[:, c0 : c0 + n].bitcast(FP8X4), rhs_scale=x2_s[:, c0 : c0 + n],
                    start=(c == 0 or c == last), stop=False,
                )

        work = []
        for c, (c0, n) in enumerate(Z_CHUNKS):
            work.append({name: new([P, PACK, n], F32, "%s%d" % (name, c)) for name in ("root", "factor")})
        den_low = keep.tile([P, PACK, half], F32, name="den_low", tag="den_then_top", align_bytes=64)

        def interleave(c):
            c0, n = Z_CHUNKS[c]
            factor = work[c]["root" if c == VECTOR_CHUNK else "factor"]
            z_bf = new([P, n, PACK], BF16, "z_bf%d" % c)
            walk = "p t (c i) -> p c t i"
            nc.vector.tensor_tensor(
                z_bf[:].rearrange("p (c i) t -> p c t i", i=4),
                work[c]["top"][:].rearrange(walk, i=4), factor[:].rearrange(walk, i=4), ALU.mult,
            )
            return z_bf

        def second_product(c, z_bf):
            c0, n = Z_CHUNKS[c]
            z_w = new([P, n], U32, "z_w%d" % c)
            z_s = new([P, n], U8, "z_s%d" % c)
            nc.vector.quantize_mx(out=z_w[:].bitcast(FP8X4), scales=z_s[:], in_=z_bf[:].rearrange("p c t -> p (c t)"))
            for t in range(PACK):
                cols = slice(t * P, (t + 1) * P)
                nc.tensor.matmul_mx(
                    out=h2_sums(c, t), lhsT=w1_dealt[:, cols].bitcast(FP8X4), lhsT_scale=w_dealt_s[:, cols],
                    rhs=z_w[:].bitcast(FP8X4), rhs_scale=z_s[:],
                    start=False, stop=(c >= last - 1),
                )

        def fetch_top(c):
            c0, n = Z_CHUNKS[c]
            for t in range(PACK):
                picked = gained[t][:].indirect(entries(lists["n1"], c0, n))
                if c == VECTOR_CHUNK:
                    nc.vector.tensor_tensor(work[c]["top"][:, t, :], picked, work[c]["root"][:, t, :], ALU.mult)
                else:
                    nc.scalar.activation(work[c]["top"][:, t, :], picked, ACT.Copy)

        def denominators(c, den, own_size):
            c0, n = Z_CHUNKS[c]
            for t in range(PACK):
                nc.vector.tensor_tensor(den[:, t, :], size[t][:].indirect(entries(lists["n2"], c0, n)), own_size[t], ALU.add)

        def roots(c, den):
            for pair in (slice(0, 2), slice(2, 4)):
                nc.scalar.activation(work[c]["root"][:, pair, :], den[:, pair, :], ACT.Abs_reciprocal_sqrt, bias=8.0)
                if c != VECTOR_CHUNK:
                    nc.scalar.activation(work[c]["factor"][:, pair, :], work[c]["root"][:, pair, :], ACT.Square)

        work[0]["top"] = new([P, PACK, half], F32, "top0")
        work[1]["top"] = new([P, PACK, half // 2], F32, "top1")
        fetch_top(0)
        denominators(0, den_low[:], [tile[:] for tile in size_low])
        den_high = keep.tile([P, 2, PACK, half // 2], F32, name="den_high", tag="low_then_den", align_bytes=64)
        den = [den_low[:], den_high[:, 0, :, :], den_high[:, 1, :, :]]
        denominators(1, den[1], [tile[:, : half // 2] for tile in size_high])
        denominators(2, den[2], [tile[:, half // 2 :] for tile in size_high])
        roots(0, den[0])
        roots(1, den[1])
        work[2]["top"] = keep.tile([P, PACK, half // 2], F32, name="top_last", tag="den_then_top", align_bytes=64)
        fetch_top(2)
        roots(2, den[2])
        z_bf = interleave(0)
        fetch_top(1)
        second_product(0, z_bf)
        second_product(1, interleave(1))

        nc.scalar.activation(warm[:, 9:10], work[last]["root"][:, PACK - 1, last_n - 1 :], ACT.Sigmoid)
        h2 = [new([P, S], F32, "h2_%d" % t) for t in range(PACK)]
        second_product(last, interleave(last))
        for t in range(PACK):
            (nc.scalar.copy if t < EARLY_ON_SCALAR else nc.vector.tensor_copy)(h2[t][:, :last_c0], early_bank[t][:])
            nc.vector.tensor_copy(h2[t][:, last_c0:], last_bank[t][:])
        y_s = new([P, S], U8, "y_s")
        out_rows = out_0.rearrange("(p t) j -> p t j", t=PACK)
        out_words = words_view(out_1)
        for c, (c0, n) in enumerate(Y_CHUNKS):
            sg = new([P, PACK, n], F32, "sg%d" % c)
            sg2 = new([P, PACK, n], F32, "sg2_%d" % c)
            diff = new([P, PACK, n], F32, "diff%d" % c)
            y = new([P, PACK, n], F32, "y%d" % c)
            y_bf = new([P, n, PACK], BF16, "y_bf%d" % c)
            y_w = new([P, n], U32, "y_w%d" % c)
            group = 1
            for t0 in range(0, PACK, group):
                for t in range(t0, t0 + group):
                    scale = sl_sb[:, t : t + 1]
                    picked = h2[t][:].indirect(entries(lists["n3"], c0, n))
                    nc.scalar.activation(sg[:, t, :], picked, ACT.Sigmoid, bias=bias_lo[:, t : t + 1], scale=scale)
                    nc.scalar.activation(sg2[:, t, :], picked, ACT.Sigmoid, bias=bias_hi[:, t : t + 1], scale=scale)
                ts = slice(t0, t0 + group)
                nc.vector.tensor_tensor(diff[:, ts, :], sg[:, ts, :], sg2[:, ts, :], ALU.subtract)
                for t in range(t0, t0 + group):
                    nc.vector.tensor_tensor(y[:, t, :], diff[:, t, :], h2[t][:, c0 : c0 + n], ALU.mult)
                    if c == len(Y_CHUNKS) - 1:
                        nc.sync.dma_start(out_rows[:, t, c0 : c0 + n], y[:, t, :])
            if c < len(Y_CHUNKS) - 1:
                nc.sync.dma_start(out_rows[:, :, c0 : c0 + n], y[:])
            nc.vector.tensor_copy(
                y_bf[:].rearrange("p (c i) t -> p c t i", i=4), y[:].rearrange("p t (c i) -> p c t i", i=4)
            )
            nc.vector.quantize_mx(
                out=y_w[:].bitcast(FP8X4), scales=y_s[:, c0 : c0 + n], in_=y_bf[:].rearrange("p c t -> p (c t)")
            )
            nc.sync.dma_start(out_words[:, c0 : c0 + n], y_w[:].bitcast(I32))
        for r in range(4):
            queue = (nc.scalar, nc.sync)[r % 2]
            queue.dma_start(out_2[0][r:16:4, :].bitcast(I32), y_s[r:P:32, :].bitcast(I32))
